import numpy as np
import ml_dtypes


def mxq(x, axis, fmt="e4m3"):
    dtype, down = {"e4m3": (ml_dtypes.float8_e4m3fn, 7), "e5m2": (ml_dtypes.float8_e5m2, 14)}[fmt]
    v = np.moveaxis(np.asarray(x, np.float32).astype(ml_dtypes.bfloat16).astype(np.float64), axis, -1)
    blocks = v.reshape(v.shape[:-1] + (-1, 32))
    amax = np.abs(blocks).max(-1, keepdims=True)
    byte = np.maximum(np.where(amax > 0, np.frexp(amax)[1] - 1 + 127, 0) - down, 1)
    scale = np.exp2(byte - 127.0)
    codes = (blocks / scale).astype(np.float32).astype(dtype).astype(np.float64)
    return np.moveaxis((codes * scale).reshape(v.shape), -1, axis)


WIDE = False


def mx_kscale(k):
    if not WIDE:
        return np.ones(k)
    levels = np.array([10, -10, 5, -5, 0])
    if k % 512:
        return np.exp2(np.random.permutation(np.resize(levels, k // 32))).repeat(32)
    a = np.empty((k // 512, 16))
    for p in range(k // 512):
        a[p, :8] = np.random.permutation(np.resize(levels, 8))
        for g in range(8):
            far = levels[np.abs(levels - a[p, g]) >= 10]
            a[p, g + 8] = far[np.random.randint(len(far))]
    return np.exp2(a.ravel()).repeat(32)


def f64(x):
    return np.asarray(x).astype(np.float64)


def striped(idx):
    return np.tile(idx.reshape(-1, 16).T, (8, 1)).astype(np.uint16)


def unstriped(offs):
    return offs[:16].T.reshape(-1).astype(np.int64)


E2M1 = np.array([0.0, 0.5, 1.0, 1.5, 2.0, 3.0, 4.0, 6.0, -0.0, -0.5, -1.0, -1.5, -2.0, -3.0, -4.0, -6.0])


def pack_weight(w, fmt):
    k, n = w.shape
    w = f64(np.asarray(w, np.float32).astype(ml_dtypes.bfloat16)).reshape(k // 32, 32, n)
    amax = np.abs(w).max(1)
    if fmt == "e4m3":
        byte = np.frexp(amax)[1] - 1 + 127 - 7
    else:
        mant, ex = np.frexp(amax / 6.0)
        byte = np.where(mant > 0.5, ex, ex - 1) + 127
    byte = np.clip(np.where(amax > 0, byte, 1), 1, 254)
    scaled = (w * np.exp2(127.0 - byte)[:, None, :]).reshape(k, n).astype(np.float32)
    by_word = np.ascontiguousarray(scaled.reshape(k // 512, 128, 4, n).transpose(0, 1, 3, 2))
    if fmt == "e4m3":
        words = by_word.astype(ml_dtypes.float8_e4m3fn).view(np.uint8)
    else:
        c = by_word.astype(ml_dtypes.float4_e2m1fn).view(np.uint8) & 0xF
        words = (c[..., 0::2] | (c[..., 1::2] << 4)).reshape(k // 512, 128, 2 * n)
    return np.ascontiguousarray(words), np.ascontiguousarray(byte.astype(np.uint8).reshape(k // 512, 16, n))


def unpack_weight(words, scales, fmt):
    g, _, n = scales.shape
    words = np.ascontiguousarray(words).reshape(g, 128, n, -1)
    if fmt == "e4m3":
        vals = words.view(ml_dtypes.float8_e4m3fn).astype(np.float64)
    else:
        nib = np.empty((g, 128, n, 4), np.uint8)
        nib[..., 0::2] = words & 0xF
        nib[..., 1::2] = words >> 4
        vals = E2M1[nib]
    vals = vals * np.repeat(np.exp2(scales.astype(np.float64) - 127.0), 8, axis=1)[..., None]
    return vals.transpose(0, 1, 3, 2).reshape(g * 512, n)


def d_silu(v):
    s = 1.0 / (1.0 + np.exp(-np.maximum(v, -700.0)))
    return s * (1.0 + v * (1.0 - s))


K, T, E, C, H, N, TOP = 128, 512, 8, 256, 512, 1024, 4


def by_expert(wq, xq):
    return np.concatenate([wq[e].T @ xq[:, e * C:(e + 1) * C] for e in range(E)], axis=1)


def setup_inputs():
    n = np.random.standard_normal
    v = mx_kscale(N)
    u = mx_kscale(H)
    deal = np.repeat(np.arange(E), C).reshape(TOP, T)[:, np.random.permutation(T)]
    deal = np.take_along_axis(deal, np.argsort(np.random.rand(TOP, T), axis=0), axis=0)
    for _ in range(8):
        s_, t_ = np.random.permutation(T).reshape(2, -1); r = np.random.randint(TOP, size=T // 2); x, y = deal[r, s_].copy(), deal[r, t_].copy()
        ok = ~((deal[:, s_] == y).any(0) | (deal[:, t_] == x).any(0)); deal[r[ok], s_[ok]] = y[ok]; deal[r[ok], t_[ok]] = x[ok]
    order = np.lexsort((np.random.rand(TOP * T), deal.reshape(-1)))
    slot_token = order % T; pos = np.empty(TOP * T, np.int64); pos[order] = np.arange(TOP * T); pos = pos.reshape(TOP, T)
    g = np.random.uniform(0.5, 1.5, (TOP, T)); g = g / g.sum(0)
    dy = pack_weight(n((N, T)) * v[:, None], "e4m3")
    return {
        "dy_words": dy[0],
        "dy_scales": dy[1],
        "w2t": (n((E, N, H)) / np.sqrt(N) / v[None, :, None] * u).astype(np.float32),
        "w1t": (n((H, K)) / np.sqrt(H) / u[:, None]).astype(np.float32),
        "a": (n((H, T))).astype(np.float32),
        "gate": np.stack([np.tile(r, (128, 1)) for r in g]).astype(np.float32),
        "offs": striped(slot_token),
        "pos1": striped(pos[0]),
        "pos2": striped(pos[1]),
        "pos3": striped(pos[2]),
        "pos4": striped(pos[3]),
    }


def reference(dy_words, dy_scales, w2t, w1t, a, gate, offs, pos1, pos2, pos3, pos4):
    w2tq = mxq(f64(w2t), 1, "e4m3")
    w1tq = mxq(f64(w1t), 0, "e4m3")
    idx = unstriped(offs)
    gq = unpack_weight(dy_words, dy_scales, "e4m3")[:, idx]
    y = by_expert(w2tq, gq)
    dh = sum(f64(gate[r, :1]) * y[:, unstriped(p)] for r, p in enumerate((pos1, pos2, pos3, pos4)))
    return w1tq.T @ mxq(dh * d_silu(f64(a)), 0, "e4m3")

@@ -1,0 +1,249 @@
+from contextlib import ExitStack
+
+import concourse.mybir as mybir
+from concourse.masks import make_identity
+
+K, T, E, C, H, N, TOP = 128, 512, 8, 256, 512, 1024, 4
+S = E * C
+FLOPS = 2 * N * H * S + 2 * H * K * T
+
+F32 = mybir.dt.float32
+BF16 = mybir.dt.bfloat16
+I32 = mybir.dt.int32
+U32 = mybir.dt.uint32
+U16 = mybir.dt.uint16
+U8 = mybir.dt.uint8
+FP8X4 = mybir.dt.float8_e4m3fn_x4
+MULT = mybir.AluOpType.mult
+SUB = mybir.AluOpType.subtract
+SIGMOID = mybir.ActivationFunctionType.Sigmoid
+
+P = 128
+PASSES = N // (4 * P)
+BLOCKS = H // P
+STEPS = BLOCKS * E
+LAST = STEPS - 1
+SPARE = 256
+SLOT = 4 * PASSES * P * 4
+HALF = SLOT // 2
+FIRST_LAG = 2
+EMPTY_LAG = 3
+COMBINE_AT = 4
+SLOPE_AT = 9
+VECTOR_CAST_EXPERTS = (2,)
+LAST_PIECE = 128
+
+
+def tile_moe_sub_silu_kernel(
+    tc, dy_words, dy_scales, w2t, w1t, a, gate, offs, pos1, pos2, pos3, pos4, out
+):
+    nc = tc.nc
+    with ExitStack() as ctx:
+        keep = ctx.enter_context(tc.tile_pool(name="keep", bufs=1))
+        stage = ctx.enter_context(tc.tile_pool(name="stage", bufs=1))
+        ring = ctx.enter_context(tc.tile_pool(name="ring", bufs=1))
+        psum = ctx.enter_context(tc.psum_pool(name="psum", bufs=1))
+
+        def over(step, start, shape, dtype, name):
+            return stage.tile(shape, dtype, name=name, offset=SLOT * step + start, align_bytes=64)
+
+        offs_sb = keep.tile([P, S // 16], U16, name="offs_sb")
+        pos_sb = [keep.tile([P, T // 16], U16, name="pos_sb%d" % r) for r in range(TOP)]
+        words = keep.tile([P, PASSES * T + SPARE], I32, name="words", align_bytes=64)
+        planes = keep.tile([P, 2 * T], U8, name="planes", align_bytes=64)
+        ident = keep.tile([P, P], F32, name="ident")
+        gates = [keep.tile([P, T], F32, name="gates%d" % r) for r in range(TOP)]
+        a_sb = [keep.tile([P, T], F32, name="a_sb%d" % b) for b in range(BLOCKS)]
+        w1_raw = keep.tile([P, 4, K], F32, name="w1_raw")
+        da_t = keep.tile([P, T // P, H], BF16, name="da_t", align_bytes=64)
+        raw = [over(n, 0, [P, 4, PASSES, P], F32, "raw%d" % n) for n in range(STEPS)]
+
+        make_identity(nc, ident[:])
+        nc.vector.memset(planes[:].bitcast(I32), 0)
+        nc.vector.memset(words[:, PASSES * T :], 0)
+
+        nc.sync.dma_start(offs_sb[:], offs)
+        nc.sync.dma_start(
+            words[:, : PASSES * T].rearrange("p (s t) -> p s t", s=PASSES),
+            dy_words.rearrange("s p t d -> p s (t d)").bitcast(I32),
+        )
+        for n in range(STEPS):
+            b, e = divmod(n, E)
+            for s in range(PASSES):
+                rows = w2t[e, 4 * P * s : 4 * P * (s + 1), P * b : P * (b + 1)]
+                nc.sync.dma_start(raw[n][:, :, s, :], rows.rearrange("(p j) w -> p j w", j=4))
+            if n == 0:
+                for q in range(4):
+                    nc.sync.dma_start(
+                        planes[32 * q : 32 * q + 4 * PASSES, :T].bitcast(I32),
+                        dy_scales[:, 4 * q : 4 * (q + 1), :].bitcast(I32),
+                    )
+            if e == 2:
+                nc.sync.dma_start(a_sb[b][:], a[P * b : P * (b + 1), :])
+            if n == E + 2:
+                for r, pos in enumerate((pos1, pos2, pos3, pos4)):
+                    nc.sync.dma_start(pos_sb[r][:], pos)
+                for r in range(TOP):
+                    nc.sync.dma_start(gates[r][:], gate[r])
+            if n == 2 * E + 2:
+                nc.sync.dma_start(w1_raw[:], w1t.rearrange("(p j) k -> p j k", j=4))
+
+        def interleave(engine_copy, dst, src):
+            engine_copy(
+                dst.rearrange("p (c i) j -> p c j i", i=2),
+                src.rearrange("p j (c i) -> p c j i", i=2),
+            )
+
+        slopes = {}
+
+        def slope(b, u):
+            a_t = psum.tile([P, T // P, P], F32, name="a_t", tag="turn", bufs=2)
+            for tb in range(T // P):
+                nc.tensor.transpose(a_t[:, tb, :], a_sb[b][:, P * tb : P * (tb + 1)], ident[:])
+            v = a_t[:].rearrange("p b i -> p (b i)")
+            sg = ring.tile([P, T], F32, name="sg", tag="sg", bufs=2)
+            nc.scalar.activation(sg[:], v, SIGMOID)
+            nc.vector.scalar_tensor_tensor(u[:], sg[:], 1.0, v, SUB, MULT)
+            neg = ring.tile([P, T // P, P], F32, name="neg", tag="neg", bufs=2)
+            nc.vector.scalar_tensor_tensor(neg[:].rearrange("p b i -> p (b i)"), u[:], 1.0, sg[:], SUB, MULT)
+            slopes[b] = neg
+
+        g_words = {}
+        g_planes = {}
+
+        def gather_words(k, s, dst):
+            window = words[:, T * s : T * (s + 1) + SPARE].bitcast(U32)
+            nc.vector.tensor_copy(dst[:], window.indirect(offs_sb[:, 32 * k : 32 * (k + 1)]))
+            g_words[k, s] = dst
+
+        def gather_planes(k, dst):
+            nc.vector.tensor_copy(dst[:], planes[:].indirect(offs_sb[:, 32 * k : 32 * (k + 1)]))
+            g_planes[k] = dst
+
+        grouped = {}
+
+        def cast(n):
+            b, e = divmod(n, E)
+            dst = ring.tile([P, PASSES * P, 4], BF16, name="grouped", tag="grouped", bufs=8, align_bytes=64)
+            engine_copy = nc.vector.tensor_copy if (b > 0 and e in VECTOR_CAST_EXPERTS) else nc.scalar.copy
+            interleave(engine_copy, dst[:], raw[n][:].rearrange("p j s w -> p j (s w)"))
+            grouped[n] = dst
+
+        def quantize(src, cols, tag, bufs, scales=None):
+            codes = ring.tile([P, cols], U32, name="codes", tag="codes" + tag, bufs=bufs, align_bytes=64)
+            if scales is None:
+                scales = ring.tile([P, cols], U8, name="scales", tag="scales" + tag, bufs=bufs, align_bytes=64)
+            nc.vector.quantize_mx(codes[:].bitcast(FP8X4), scales[:], src)
+            return codes, scales
+
+        accs = {}
+
+        def expert(n, scales):
+            k, half = divmod(n % E, 2)
+            codes, scales = quantize(grouped[n][:].rearrange("p w j -> p (w j)"), PASSES * P, "w2", 4, scales)
+            if half == 0:
+                accs[n // 2] = psum.tile([P, 2 * C], F32, name="acc", tag="acc", bufs=4)
+            slots = slice(C * half, C * (half + 1))
+            for s in range(PASSES):
+                cols = slice(P * s, P * (s + 1))
+                nc.tensor.matmul_mx(
+                    accs[n // 2][:, slots],
+                    lhsT=codes[:, cols].bitcast(FP8X4),
+                    lhsT_scale=scales[:, cols],
+                    rhs=g_words[k, s][:, slots].bitcast(FP8X4),
+                    rhs_scale=g_planes[k][4 * s :, slots],
+                    start=(s == 0),
+                    stop=(s == PASSES - 1),
+                )
+
+        ys = {}
+
+        def empty(pair):
+            b, k = divmod(pair, E // 2)
+            if k == 0:
+                ys[b] = ring.tile([P, S], F32, name="y", tag="y", bufs=2)
+            nc.scalar.copy(ys[b][:, 2 * C * k : 2 * C * (k + 1)], accs[pair][:])
+
+        def fetch(b, r, t0, nt, prod):
+            nc.vector.tensor_tensor(
+                prod[:], ys[b][:].indirect(pos_sb[r][:, t0 // 16 : (t0 + nt) // 16]), gates[r][:, t0 : t0 + nt], MULT
+            )
+
+        def combine(b, t0, nt, prods):
+            dh = psum.tile([P, nt // P, P], F32, name="dh", tag="turn", bufs=2)
+            for tb in range(nt // P):
+                for r in range(TOP):
+                    nc.tensor.matmul(
+                        dh[:, tb, :], prods[r][:, P * tb : P * (tb + 1)], ident[:],
+                        start=(r == 0), stop=(r == TOP - 1), is_transpose=True,
+                    )
+            blocks = slice(t0 // P, (t0 + nt) // P)
+            nc.vector.scalar_tensor_tensor(
+                da_t[:, blocks, P * b : P * (b + 1)], dh[:], -1.0, slopes[b][:, blocks, :], MULT, MULT
+            )
+
+        def finish(t0, nt, w1_codes, w1_scales):
+            back = psum.tile([P, nt // P, 2, P], F32, name="back", tag="back", bufs=2)
+            for tb in range(nt // P):
+                pairs = da_t[:, t0 // P + tb, :].bitcast(F32)
+                for u in range(2):
+                    nc.tensor.transpose(back[:, tb, u, :], pairs[:, u::2], ident[:])
+            da = ring.tile([P, nt // P, P, 4], BF16, name="da", tag="da", bufs=2, align_bytes=64)
+            flat = da[:].rearrange("p b t j -> p (b t j)")
+            nc.scalar.copy(
+                flat.bitcast(F32).rearrange("p (b t u) -> p b t u", u=2, t=P), back[:].rearrange("p b u t -> p b t u")
+            )
+            codes, scales = quantize(flat, nt, "da", 2)
+            res = psum.tile([P, nt], F32, name="res", tag="acc", bufs=4)
+            nc.tensor.matmul_mx(
+                res[:], lhsT=w1_codes[:].bitcast(FP8X4), lhsT_scale=w1_scales[:],
+                rhs=codes[:].bitcast(FP8X4), rhs_scale=scales[:], start=True, stop=True,
+            )
+            res_sb = ring.tile([P, nt], F32, name="res_sb", tag="res_sb", bufs=4)
+            nc.scalar.copy(res_sb[:], res[:])
+            nc.sync.dma_start(out[:, t0 : t0 + nt], res_sb[:])
+
+        for k in range(2):
+            for s in range(PASSES):
+                gather_words(k, s, keep.tile([P, 2 * C], U32, name="g_words%d_%d" % (k, s), align_bytes=64))
+            gather_planes(k, keep.tile([P, 2 * C], U8, name="g_planes%d" % k, align_bytes=64))
+
+        quantize_at = [max(n, min(n + FIRST_LAG, E - 1 + FIRST_LAG)) for n in range(STEPS)]
+        empty_at = [min(LAST, max(2 * pair + 1 + EMPTY_LAG, quantize_at[2 * pair + 1])) for pair in range(STEPS // 2)]
+        prods = {}
+        w1q = []
+        for m in range(STEPS):
+            cast(m)
+            for n in range(STEPS):
+                if quantize_at[n] == m:
+                    held = over(m, 256 * (n % 4), [P, PASSES * P], U8, "scales%d" % n) if n < m else None
+                    expert(n, held)
+            for k in (2, 3):
+                if m == 2 * k - 1:
+                    gather_words(k, 0, over(m, HALF, [P, 2 * C], U32, "g_words%d_0" % k))
+                    gather_planes(k, over(m, 1024, [P, 2 * C], U8, "g_planes%d" % k))
+                if m == 2 * k:
+                    gather_words(k, 1, over(m, HALF, [P, 2 * C], U32, "g_words%d_1" % k))
+            for pair in range(STEPS // 2):
+                if empty_at[pair] == m:
+                    empty(pair)
+            b, r = divmod(m - E - COMBINE_AT, E)
+            if b >= 0 and r < TOP:
+                prods[r] = over(m, 0, [P, T], F32, "prod%d" % m)
+                fetch(b, r, 0, T, prods[r])
+            for bb in range(BLOCKS):
+                if min(LAST, E * bb + SLOPE_AT) == m:
+                    slope(bb, over(m, HALF, [P, T], F32, "u%d" % bb))
+            if b >= 0 and r == TOP - 1:
+                combine(b, 0, T, prods)
+            if m == 2 * E + 4:
+                w1_grouped = keep.tile([P, K, 4], BF16, name="w1_grouped", align_bytes=64)
+                interleave(nc.vector.tensor_copy, w1_grouped[:], w1_raw[:])
+                w1q.extend(quantize(w1_grouped[:].rearrange("p k j -> p (k j)"), K, "w1", 1))
+
+        for t0 in range(0, T, LAST_PIECE):
+            for r in range(TOP):
+                prods[r] = ring.tile([P, LAST_PIECE], F32, name="last_prod", tag="last_prod", bufs=TOP * T // LAST_PIECE)
+                fetch(BLOCKS - 1, r, t0, LAST_PIECE, prods[r])
+            combine(BLOCKS - 1, t0, LAST_PIECE, prods)
+            finish(t0, LAST_PIECE, w1q[0], w1q[1])

@@ -21,16 +21,16 @@ SIGMOID = mybir.ActivationFunctionType.Sigmoid
 P = 128
 PASSES = N // (4 * P)
 BLOCKS = H // P
-STEPS = BLOCKS * E
-LAST = STEPS - 1
 SPARE = 256
-SLOT = 4 * PASSES * P * 4
-HALF = SLOT // 2
-FIRST_LAG = 2
-EMPTY_LAG = 3
-COMBINE_AT = 4
-SLOPE_AT = 9
-VECTOR_CAST_EXPERTS = (2,)
+WIDE = 6
+UNITS = [(e, s, h) for e in range(WIDE) for s in range(PASSES) for h in range(2)]
+UNITS = UNITS + [(e, None, b) for b in range(BLOCKS) for e in range(WIDE, E)]
+FIRST_NARROW = 4 * WIDE
+LAST = len(UNITS) - 1
+UNIT_BYTES = 4096
+ROOM = 2048
+VECTOR_CASTS = range(7, FIRST_NARROW + 2, 2)
+SLOPE_FROM = 4
 LAST_PIECE = 128
 
 
@@ -44,19 +44,17 @@ def tile_moe_sub_silu_kernel(
         ring = ctx.enter_context(tc.tile_pool(name="ring", bufs=1))
         psum = ctx.enter_context(tc.psum_pool(name="psum", bufs=1))
 
-        def over(step, start, shape, dtype, name):
-            return stage.tile(shape, dtype, name=name, offset=SLOT * step + start, align_bytes=64)
+        def over(unit, room, shape, dtype, name):
+            return stage.tile(shape, dtype, name=name, offset=UNIT_BYTES * unit + ROOM * room, align_bytes=64)
 
         offs_sb = keep.tile([P, S // 16], U16, name="offs_sb")
         pos_sb = [keep.tile([P, T // 16], U16, name="pos_sb%d" % r) for r in range(TOP)]
         words = keep.tile([P, PASSES * T + SPARE], I32, name="words", align_bytes=64)
         planes = keep.tile([P, 2 * T], U8, name="planes", align_bytes=64)
         ident = keep.tile([P, P], F32, name="ident")
-        gates = [keep.tile([P, T], F32, name="gates%d" % r) for r in range(TOP)]
         a_sb = [keep.tile([P, T], F32, name="a_sb%d" % b) for b in range(BLOCKS)]
         w1_raw = keep.tile([P, 4, K], F32, name="w1_raw")
         da_t = keep.tile([P, T // P, H], BF16, name="da_t", align_bytes=64)
-        raw = [over(n, 0, [P, 4, PASSES, P], F32, "raw%d" % n) for n in range(STEPS)]
 
         make_identity(nc, ident[:])
         nc.vector.memset(planes[:].bitcast(I32), 0)
@@ -67,36 +65,49 @@ def tile_moe_sub_silu_kernel(
             words[:, : PASSES * T].rearrange("p (s t) -> p s t", s=PASSES),
             dy_words.rearrange("s p t d -> p s (t d)").bitcast(I32),
         )
-        for n in range(STEPS):
-            b, e = divmod(n, E)
-            for s in range(PASSES):
-                rows = w2t[e, 4 * P * s : 4 * P * (s + 1), P * b : P * (b + 1)]
-                nc.sync.dma_start(raw[n][:, :, s, :], rows.rearrange("(p j) w -> p j w", j=4))
+        raw = {}
+
+        def load(n):
+            e, s, h = UNITS[n]
+            if s is None:
+                raw[n] = over(n, 0, [P, 4, PASSES, P], F32, "raw%d" % n)
+                for t in range(PASSES):
+                    rows = w2t[e, 4 * P * t : 4 * P * (t + 1), P * h : P * (h + 1)]
+                    nc.sync.dma_start(raw[n][:, :, t, :], rows.rearrange("(p j) w -> p j w", j=4))
+            elif h == 0:
+                raw[n] = over(n, 0, [P, 4, H], F32, "raw%d" % n)
+                rows = w2t[e, 4 * P * s : 4 * P * (s + 1), :]
+                nc.sync.dma_start(raw[n][:], rows.rearrange("(p j) w -> p j w", j=4))
             if n == 0:
                 for q in range(4):
                     nc.sync.dma_start(
                         planes[32 * q : 32 * q + 4 * PASSES, :T].bitcast(I32),
                         dy_scales[:, 4 * q : 4 * (q + 1), :].bitcast(I32),
                     )
-            if e == 2:
+            b = n // 2 - SLOPE_FROM + 1
+            if n % 2 == 0 and 0 <= b < BLOCKS:
                 nc.sync.dma_start(a_sb[b][:], a[P * b : P * (b + 1), :])
-            if n == E + 2:
-                for r, pos in enumerate((pos1, pos2, pos3, pos4)):
-                    nc.sync.dma_start(pos_sb[r][:], pos)
-                for r in range(TOP):
-                    nc.sync.dma_start(gates[r][:], gate[r])
-            if n == 2 * E + 2:
+            if n == FIRST_NARROW - 4:
                 nc.sync.dma_start(w1_raw[:], w1t.rearrange("(p j) k -> p j k", j=4))
+
+        gates = []
+
+        def load_gates():
+            for r, pos in enumerate((pos1, pos2, pos3, pos4)):
+                nc.sync.dma_start(pos_sb[r][:], pos)
+            for r in range(TOP):
+                gates.append(over(16, r, [P, T], F32, "gates%d" % r))
+                nc.sync.dma_start(gates[r][:], gate[r])
 
         def interleave(engine_copy, dst, src):
             engine_copy(
-                dst.rearrange("p (c i) j -> p c j i", i=2),
-                src.rearrange("p j (c i) -> p c j i", i=2),
+                dst.rearrange("p (c i) j -> p c j i", i=4),
+                src.rearrange("p j (c i) -> p c j i", i=4),
             )
 
         slopes = {}
 
-        def slope(b, u):
+        def slope(b, u, neg):
             a_t = psum.tile([P, T // P, P], F32, name="a_t", tag="turn", bufs=2)
             for tb in range(T // P):
                 nc.tensor.transpose(a_t[:, tb, :], a_sb[b][:, P * tb : P * (tb + 1)], ident[:])
@@ -104,7 +115,6 @@ def tile_moe_sub_silu_kernel(
             sg = ring.tile([P, T], F32, name="sg", tag="sg", bufs=2)
             nc.scalar.activation(sg[:], v, SIGMOID)
             nc.vector.scalar_tensor_tensor(u[:], sg[:], 1.0, v, SUB, MULT)
-            neg = ring.tile([P, T // P, P], F32, name="neg", tag="neg", bufs=2)
             nc.vector.scalar_tensor_tensor(neg[:].rearrange("p b i -> p (b i)"), u[:], 1.0, sg[:], SUB, MULT)
             slopes[b] = neg
 
@@ -123,31 +133,35 @@ def tile_moe_sub_silu_kernel(
         grouped = {}
 
         def cast(n):
-            b, e = divmod(n, E)
-            dst = ring.tile([P, PASSES * P, 4], BF16, name="grouped", tag="grouped", bufs=8, align_bytes=64)
-            engine_copy = nc.vector.tensor_copy if (b > 0 and e in VECTOR_CAST_EXPERTS) else nc.scalar.copy
-            interleave(engine_copy, dst[:], raw[n][:].rearrange("p j s w -> p j (s w)"))
+            e, s, h = UNITS[n]
+            dst = ring.tile([P, 2 * P, 4], BF16, name="grouped", tag="grouped", bufs=8, align_bytes=64)
+            engine_copy = nc.vector.tensor_copy if n in VECTOR_CASTS else nc.scalar.copy
+            if s is None:
+                src = raw[n][:].rearrange("p j s w -> p j (s w)")
+            else:
+                src = raw[n - h][:, :, 2 * P * h : 2 * P * (h + 1)]
+            interleave(engine_copy, dst[:], src)
             grouped[n] = dst
 
-        def quantize(src, cols, tag, bufs, scales=None):
+        def quantize(src, cols, tag, bufs):
             codes = ring.tile([P, cols], U32, name="codes", tag="codes" + tag, bufs=bufs, align_bytes=64)
-            if scales is None:
-                scales = ring.tile([P, cols], U8, name="scales", tag="scales" + tag, bufs=bufs, align_bytes=64)
+            scales = ring.tile([P, cols], U8, name="scales", tag="scales" + tag, bufs=bufs, align_bytes=64)
             nc.vector.quantize_mx(codes[:].bitcast(FP8X4), scales[:], src)
             return codes, scales
 
         accs = {}
+        ys = [keep.tile([P, S], F32, name="y%d" % b) for b in range(BLOCKS)]
 
-        def expert(n, scales):
-            k, half = divmod(n % E, 2)
-            codes, scales = quantize(grouped[n][:].rearrange("p w j -> p (w j)"), PASSES * P, "w2", 4, scales)
+        def expert(e, b, operands):
+            k, half = divmod(e, 2)
             if half == 0:
-                accs[n // 2] = psum.tile([P, 2 * C], F32, name="acc", tag="acc", bufs=4)
+                accs[k, b] = psum.tile([P, 2 * C], F32, name="acc", tag="acc", bufs=6)
             slots = slice(C * half, C * (half + 1))
             for s in range(PASSES):
-                cols = slice(P * s, P * (s + 1))
+                codes, scales, col = operands[s]
+                cols = slice(P * col, P * (col + 1))
                 nc.tensor.matmul_mx(
-                    accs[n // 2][:, slots],
+                    accs[k, b][:, slots],
                     lhsT=codes[:, cols].bitcast(FP8X4),
                     lhsT_scale=scales[:, cols],
                     rhs=g_words[k, s][:, slots].bitcast(FP8X4),
@@ -155,14 +169,19 @@ def tile_moe_sub_silu_kernel(
                     start=(s == 0),
                     stop=(s == PASSES - 1),
                 )
+            if half == 1:
+                nc.scalar.copy(ys[b][:, 2 * C * k : 2 * C * (k + 1)], accs[k, b][:])
 
-        ys = {}
+        quantized = {}
 
-        def empty(pair):
-            b, k = divmod(pair, E // 2)
-            if k == 0:
-                ys[b] = ring.tile([P, S], F32, name="y", tag="y", bufs=2)
-            nc.scalar.copy(ys[b][:, 2 * C * k : 2 * C * (k + 1)], accs[pair][:])
+        def multiply(n):
+            e, s, h = UNITS[n]
+            quantized[n] = quantize(grouped[n][:].rearrange("p w j -> p (w j)"), 2 * P, "w2", 6)
+            if s is None:
+                expert(e, h, [quantized[n] + (t,) for t in range(PASSES)])
+            elif s == PASSES - 1:
+                for i in range(2):
+                    expert(e, 2 * h + i, [quantized[n - 2] + (i,), quantized[n] + (i,)])
 
         def fetch(b, r, t0, nt, prod):
             nc.vector.tensor_tensor(
@@ -183,7 +202,7 @@ def tile_moe_sub_silu_kernel(
             )
 
         def finish(t0, nt, w1_codes, w1_scales):
-            back = psum.tile([P, nt // P, 2, P], F32, name="back", tag="back", bufs=2)
+            back = psum.tile([P, nt // P, 2, P], F32, name="back", tag="acc", bufs=6)
             for tb in range(nt // P):
                 pairs = da_t[:, t0 // P + tb, :].bitcast(F32)
                 for u in range(2):
@@ -194,7 +213,7 @@ def tile_moe_sub_silu_kernel(
                 flat.bitcast(F32).rearrange("p (b t u) -> p b t u", u=2, t=P), back[:].rearrange("p b u t -> p b t u")
             )
             codes, scales = quantize(flat, nt, "da", 2)
-            res = psum.tile([P, nt], F32, name="res", tag="acc", bufs=4)
+            res = psum.tile([P, nt], F32, name="res", tag="acc", bufs=6)
             nc.tensor.matmul_mx(
                 res[:], lhsT=w1_codes[:].bitcast(FP8X4), lhsT_scale=w1_scales[:],
                 rhs=codes[:].bitcast(FP8X4), rhs_scale=scales[:], start=True, stop=True,
@@ -203,47 +222,55 @@ def tile_moe_sub_silu_kernel(
             nc.scalar.copy(res_sb[:], res[:])
             nc.sync.dma_start(out[:, t0 : t0 + nt], res_sb[:])
 
-        for k in range(2):
-            for s in range(PASSES):
-                gather_words(k, s, keep.tile([P, 2 * C], U32, name="g_words%d_%d" % (k, s), align_bytes=64))
-            gather_planes(k, keep.tile([P, 2 * C], U8, name="g_planes%d" % k, align_bytes=64))
+        for n in range(FIRST_NARROW - 2):
+            load(n)
+        for s in range(PASSES):
+            gather_words(0, s, keep.tile([P, 2 * C], U32, name="g_words0_%d" % s, align_bytes=64))
+        gather_planes(0, keep.tile([P, 2 * C], U8, name="g_planes0", align_bytes=64))
 
-        quantize_at = [max(n, min(n + FIRST_LAG, E - 1 + FIRST_LAG)) for n in range(STEPS)]
-        empty_at = [min(LAST, max(2 * pair + 1 + EMPTY_LAG, quantize_at[2 * pair + 1])) for pair in range(STEPS // 2)]
+        narrow = E - WIDE
         prods = {}
         w1q = []
-        for m in range(STEPS):
+        for m in range(len(UNITS)):
+            if m == FIRST_NARROW - 6:
+                for n in range(FIRST_NARROW - 2, len(UNITS)):
+                    load(n)
+                    if n == FIRST_NARROW + narrow - 1:
+                        load_gates()
             cast(m)
-            for n in range(STEPS):
-                if quantize_at[n] == m:
-                    held = over(m, 256 * (n % 4), [P, PASSES * P], U8, "scales%d" % n) if n < m else None
-                    expert(n, held)
-            for k in (2, 3):
-                if m == 2 * k - 1:
-                    gather_words(k, 0, over(m, HALF, [P, 2 * C], U32, "g_words%d_0" % k))
-                    gather_planes(k, over(m, 1024, [P, 2 * C], U8, "g_planes%d" % k))
-                if m == 2 * k:
-                    gather_words(k, 1, over(m, HALF, [P, 2 * C], U32, "g_words%d_1" % k))
-            for pair in range(STEPS // 2):
-                if empty_at[pair] == m:
-                    empty(pair)
-            b, r = divmod(m - E - COMBINE_AT, E)
-            if b >= 0 and r < TOP:
-                prods[r] = over(m, 0, [P, T], F32, "prod%d" % m)
-                fetch(b, r, 0, T, prods[r])
-            for bb in range(BLOCKS):
-                if min(LAST, E * bb + SLOPE_AT) == m:
-                    slope(bb, over(m, HALF, [P, T], F32, "u%d" % bb))
-            if b >= 0 and r == TOP - 1:
-                combine(b, 0, T, prods)
-            if m == 2 * E + 4:
+            multiply(m)
+            for k in range(1, E // 2):
+                if m == 4 * k - 3:
+                    gather_words(k, 0, over(m - 1, 0, [P, 2 * C], U32, "g_words%d_0" % k))
+                    gather_planes(k, over(m - 1, 1, [P, 2 * C], U8, "g_planes%d" % k))
+                if m == 4 * k - 1:
+                    gather_words(k, 1, over(m - 1, 0, [P, 2 * C], U32, "g_words%d_1" % k))
+            b = m // 2 - SLOPE_FROM
+            if m % 2 == 1 and 0 <= b < BLOCKS:
+                slope(b, over(m - 1, 2, [P, T], F32, "u%d" % b), over(m - 1, 3, [P, T // P, P], F32, "neg%d" % b))
+            if m == FIRST_NARROW - 2:
                 w1_grouped = keep.tile([P, K, 4], BF16, name="w1_grouped", align_bytes=64)
                 interleave(nc.vector.tensor_copy, w1_grouped[:], w1_raw[:])
                 w1q.extend(quantize(w1_grouped[:].rearrange("p k j -> p (k j)"), K, "w1", 1))
+            done, rest = divmod(m + 1 - FIRST_NARROW, narrow)
+            if m >= FIRST_NARROW and rest == 0:
+                if done >= 2:
+                    b = done - 2
+                    for r in range(2, TOP):
+                        prods[b, r] = over(m, r - 2, [P, T], F32, "prod%d_%d" % (b, r))
+                        fetch(b, r, 0, T, prods[b, r])
+                    combine(b, 0, T, [prods[b, r] for r in range(TOP)])
+                b = done - 1
+                if b < BLOCKS - 1:
+                    for r in range(2):
+                        prods[b, r] = over(20, 2 * (b % 2) + r, [P, T], F32, "prod%d_%d" % (b, r))
+                        fetch(b, r, 0, T, prods[b, r])
 
         for t0 in range(0, T, LAST_PIECE):
+            last = []
             for r in range(TOP):
-                prods[r] = ring.tile([P, LAST_PIECE], F32, name="last_prod", tag="last_prod", bufs=TOP * T // LAST_PIECE)
-                fetch(BLOCKS - 1, r, t0, LAST_PIECE, prods[r])
-            combine(BLOCKS - 1, t0, LAST_PIECE, prods)
+                place = UNIT_BYTES * 18 + 4 * (T * r + t0)
+                last.append(stage.tile([P, LAST_PIECE], F32, name="last%d_%d" % (t0, r), offset=place, align_bytes=64))
+                fetch(BLOCKS - 1, r, t0, LAST_PIECE, last[r])
+            combine(BLOCKS - 1, t0, LAST_PIECE, last)
             finish(t0, LAST_PIECE, w1q[0], w1q[1])

@@ -22,16 +22,17 @@ P = 128
 PASSES = N // (4 * P)
 BLOCKS = H // P
 SPARE = 256
-WIDE = 6
-UNITS = [(e, s, h) for e in range(WIDE) for s in range(PASSES) for h in range(2)]
-UNITS = UNITS + [(e, None, b) for b in range(BLOCKS) for e in range(WIDE, E)]
-FIRST_NARROW = 4 * WIDE
-LAST = len(UNITS) - 1
-UNIT_BYTES = 4096
+WIDE = 4
+PROMPT = 2
+NARROW = E - WIDE
 ROOM = 2048
-VECTOR_CASTS = range(7, FIRST_NARROW + 2, 2)
-SLOPE_FROM = 4
+EMPTY_LAG = 2
 LAST_PIECE = 128
+FIRST = [(e, s, h) for e in range(WIDE) for s in range(PASSES) for h in range(2) if h == 0 or e < PROMPT]
+LATER = [(e, s, 1) for e in range(PROMPT, WIDE) for s in range(PASSES)]
+BY_BLOCK = [[(e, None, b) for e in range(WIDE, E)] for b in range(BLOCKS)]
+UNITS = FIRST + BY_BLOCK[0] + LATER + BY_BLOCK[1] + BY_BLOCK[2] + BY_BLOCK[3]
+VECTOR_CASTS = BY_BLOCK[0][::2]
 
 
 def tile_moe_sub_silu_kernel(
@@ -44,60 +45,64 @@ def tile_moe_sub_silu_kernel(
         ring = ctx.enter_context(tc.tile_pool(name="ring", bufs=1))
         psum = ctx.enter_context(tc.psum_pool(name="psum", bufs=1))
 
+        def place(unit):
+            e, s, h = unit
+            if s is None:
+                return 4 * ROOM * PASSES * WIDE + 2 * ROOM * (NARROW * h + e - WIDE)
+            return 4 * ROOM * (PASSES * e + s)
+
         def over(unit, room, shape, dtype, name):
-            return stage.tile(shape, dtype, name=name, offset=UNIT_BYTES * unit + ROOM * room, align_bytes=64)
+            return stage.tile(shape, dtype, name=name, offset=place(unit) + ROOM * room, align_bytes=64)
 
         offs_sb = keep.tile([P, S // 16], U16, name="offs_sb")
         pos_sb = [keep.tile([P, T // 16], U16, name="pos_sb%d" % r) for r in range(TOP)]
-        words = keep.tile([P, PASSES * T + SPARE], I32, name="words", align_bytes=64)
+        words = [keep.tile([P, T + SPARE], I32, name="words%d" % s, align_bytes=64) for s in range(PASSES)]
         planes = keep.tile([P, 2 * T], U8, name="planes", align_bytes=64)
         ident = keep.tile([P, P], F32, name="ident")
+        gates = [keep.tile([P, T], F32, name="gates%d" % r) for r in range(TOP)]
         a_sb = [keep.tile([P, T], F32, name="a_sb%d" % b) for b in range(BLOCKS)]
         w1_raw = keep.tile([P, 4, K], F32, name="w1_raw")
         da_t = keep.tile([P, T // P, H], BF16, name="da_t", align_bytes=64)
 
         make_identity(nc, ident[:])
         nc.vector.memset(planes[:].bitcast(I32), 0)
-        nc.vector.memset(words[:, PASSES * T :], 0)
+        for s in range(PASSES):
+            nc.vector.memset(words[s][:, T:], 0)
 
         nc.sync.dma_start(offs_sb[:], offs)
-        nc.sync.dma_start(
-            words[:, : PASSES * T].rearrange("p (s t) -> p s t", s=PASSES),
-            dy_words.rearrange("s p t d -> p s (t d)").bitcast(I32),
-        )
+        for s in range(PASSES):
+            nc.sync.dma_start(words[s][:, :T], dy_words[s].rearrange("p t d -> p (t d)").bitcast(I32))
         raw = {}
-
-        def load(n):
-            e, s, h = UNITS[n]
-            if s is None:
-                raw[n] = over(n, 0, [P, 4, PASSES, P], F32, "raw%d" % n)
-                for t in range(PASSES):
-                    rows = w2t[e, 4 * P * t : 4 * P * (t + 1), P * h : P * (h + 1)]
-                    nc.sync.dma_start(raw[n][:, :, t, :], rows.rearrange("(p j) w -> p j w", j=4))
-            elif h == 0:
-                raw[n] = over(n, 0, [P, 4, H], F32, "raw%d" % n)
+        for e in range(WIDE):
+            for s in range(PASSES):
+                raw[e, s] = over((e, s, 0), 0, [P, 4, H], F32, "raw%d_%d" % (e, s))
                 rows = w2t[e, 4 * P * s : 4 * P * (s + 1), :]
-                nc.sync.dma_start(raw[n][:], rows.rearrange("(p j) w -> p j w", j=4))
-            if n == 0:
-                for q in range(4):
-                    nc.sync.dma_start(
-                        planes[32 * q : 32 * q + 4 * PASSES, :T].bitcast(I32),
-                        dy_scales[:, 4 * q : 4 * (q + 1), :].bitcast(I32),
-                    )
-            b = n // 2 - SLOPE_FROM + 1
-            if n % 2 == 0 and 0 <= b < BLOCKS:
-                nc.sync.dma_start(a_sb[b][:], a[P * b : P * (b + 1), :])
-            if n == FIRST_NARROW - 4:
-                nc.sync.dma_start(w1_raw[:], w1t.rearrange("(p j) k -> p j k", j=4))
-
-        gates = []
-
-        def load_gates():
-            for r, pos in enumerate((pos1, pos2, pos3, pos4)):
-                nc.sync.dma_start(pos_sb[r][:], pos)
-            for r in range(TOP):
-                gates.append(over(16, r, [P, T], F32, "gates%d" % r))
-                nc.sync.dma_start(gates[r][:], gate[r])
+                nc.sync.dma_start(raw[e, s][:], rows.rearrange("(p j) w -> p j w", j=4))
+                n = PASSES * e + s
+                if n == 0:
+                    for q in range(4):
+                        nc.sync.dma_start(
+                            planes[32 * q : 32 * q + 4 * PASSES, :T].bitcast(I32),
+                            dy_scales[:, 4 * q : 4 * (q + 1), :].bitcast(I32),
+                        )
+                b = n - 3
+                if 0 <= b < BLOCKS:
+                    nc.sync.dma_start(a_sb[b][:], a[P * b : P * (b + 1), :])
+        for b in range(BLOCKS):
+            for e in range(WIDE, E):
+                raw[e, None, b] = over((e, None, b), 0, [P, 4, PASSES, P], F32, "raw%d_b%d" % (e, b))
+                for s in range(PASSES):
+                    rows = w2t[e, 4 * P * s : 4 * P * (s + 1), P * b : P * (b + 1)]
+                    nc.sync.dma_start(raw[e, None, b][:, :, s, :], rows.rearrange("(p j) w -> p j w", j=4))
+                if (b, e) == (0, E - 1):
+                    for r, pos in enumerate((pos1, pos2, pos3, pos4)):
+                        nc.sync.dma_start(pos_sb[r][:], pos)
+                    nc.sync.dma_start(gates[0][:], gate[0])
+                if (b, e) == (1, WIDE):
+                    for r in range(1, TOP):
+                        nc.sync.dma_start(gates[r][:], gate[r])
+                if (b, e) == (1, WIDE + 1):
+                    nc.sync.dma_start(w1_raw[:], w1t.rearrange("(p j) k -> p j k", j=4))
 
         def interleave(engine_copy, dst, src):
             engine_copy(
@@ -122,7 +127,7 @@ def tile_moe_sub_silu_kernel(
         g_planes = {}
 
         def gather_words(k, s, dst):
-            window = words[:, T * s : T * (s + 1) + SPARE].bitcast(U32)
+            window = words[s][:].bitcast(U32)
             nc.vector.tensor_copy(dst[:], window.indirect(offs_sb[:, 32 * k : 32 * (k + 1)]))
             g_words[k, s] = dst
 
@@ -132,16 +137,16 @@ def tile_moe_sub_silu_kernel(
 
         grouped = {}
 
-        def cast(n):
-            e, s, h = UNITS[n]
+        def cast(unit):
+            e, s, h = unit
             dst = ring.tile([P, 2 * P, 4], BF16, name="grouped", tag="grouped", bufs=8, align_bytes=64)
-            engine_copy = nc.vector.tensor_copy if n in VECTOR_CASTS else nc.scalar.copy
+            engine_copy = nc.vector.tensor_copy if unit in VECTOR_CASTS else nc.scalar.copy
             if s is None:
-                src = raw[n][:].rearrange("p j s w -> p j (s w)")
+                src = raw[unit][:].rearrange("p j s w -> p j (s w)")
             else:
-                src = raw[n - h][:, :, 2 * P * h : 2 * P * (h + 1)]
+                src = raw[e, s][:, :, 2 * P * h : 2 * P * (h + 1)]
             interleave(engine_copy, dst[:], src)
-            grouped[n] = dst
+            grouped[unit] = dst
 
         def quantize(src, cols, tag, bufs):
             codes = ring.tile([P, cols], U32, name="codes", tag="codes" + tag, bufs=bufs, align_bytes=64)
@@ -169,19 +174,20 @@ def tile_moe_sub_silu_kernel(
                     start=(s == 0),
                     stop=(s == PASSES - 1),
                 )
-            if half == 1:
-                nc.scalar.copy(ys[b][:, 2 * C * k : 2 * C * (k + 1)], accs[k, b][:])
+
+        def empty(k, b):
+            nc.scalar.copy(ys[b][:, 2 * C * k : 2 * C * (k + 1)], accs[k, b][:])
 
         quantized = {}
 
-        def multiply(n):
-            e, s, h = UNITS[n]
-            quantized[n] = quantize(grouped[n][:].rearrange("p w j -> p (w j)"), 2 * P, "w2", 6)
+        def multiply(unit):
+            e, s, h = unit
+            quantized[unit] = quantize(grouped[unit][:].rearrange("p w j -> p (w j)"), 2 * P, "w2", 6)
             if s is None:
-                expert(e, h, [quantized[n] + (t,) for t in range(PASSES)])
+                expert(e, h, [quantized[unit] + (t,) for t in range(PASSES)])
             elif s == PASSES - 1:
                 for i in range(2):
-                    expert(e, 2 * h + i, [quantized[n - 2] + (i,), quantized[n] + (i,)])
+                    expert(e, 2 * h + i, [quantized[e, t, h] + (i,) for t in range(PASSES)])
 
         def fetch(b, r, t0, nt, prod):
             nc.vector.tensor_tensor(
@@ -222,55 +228,61 @@ def tile_moe_sub_silu_kernel(
             nc.scalar.copy(res_sb[:], res[:])
             nc.sync.dma_start(out[:, t0 : t0 + nt], res_sb[:])
 
-        for n in range(FIRST_NARROW - 2):
-            load(n)
-        for s in range(PASSES):
-            gather_words(0, s, keep.tile([P, 2 * C], U32, name="g_words0_%d" % s, align_bytes=64))
-        gather_planes(0, keep.tile([P, 2 * C], U8, name="g_planes0", align_bytes=64))
+        for k in range(2):
+            for s in range(PASSES):
+                gather_words(k, s, keep.tile([P, 2 * C], U32, name="g_words%d_%d" % (k, s), align_bytes=64))
+            gather_planes(k, keep.tile([P, 2 * C], U8, name="g_planes%d" % k, align_bytes=64))
 
-        narrow = E - WIDE
+        def gathered(unit, room, k, s):
+            gather_words(k, s, over(unit, room, [P, 2 * C], U32, "g_words%d_%d" % (k, s)))
+
+        empty_at = {}
+        for m, (e, s, h) in enumerate(UNITS):
+            if e % 2 == 1 and s is None:
+                empty_at.setdefault(m, []).append((e // 2, h))
+            if e % 2 == 1 and s == PASSES - 1:
+                empty_at.setdefault(m + EMPTY_LAG, []).extend([(e // 2, 2 * h), (e // 2, 2 * h + 1)])
+        slope_after = [(1, 1, 1), BY_BLOCK[0][0], BY_BLOCK[0][1], BY_BLOCK[0][-1]]
         prods = {}
         w1q = []
-        for m in range(len(UNITS)):
-            if m == FIRST_NARROW - 6:
-                for n in range(FIRST_NARROW - 2, len(UNITS)):
-                    load(n)
-                    if n == FIRST_NARROW + narrow - 1:
-                        load_gates()
-            cast(m)
-            multiply(m)
-            for k in range(1, E // 2):
-                if m == 4 * k - 3:
-                    gather_words(k, 0, over(m - 1, 0, [P, 2 * C], U32, "g_words%d_0" % k))
-                    gather_planes(k, over(m - 1, 1, [P, 2 * C], U8, "g_planes%d" % k))
-                if m == 4 * k - 1:
-                    gather_words(k, 1, over(m - 1, 0, [P, 2 * C], U32, "g_words%d_1" % k))
-            b = m // 2 - SLOPE_FROM
-            if m % 2 == 1 and 0 <= b < BLOCKS:
-                slope(b, over(m - 1, 2, [P, T], F32, "u%d" % b), over(m - 1, 3, [P, T // P, P], F32, "neg%d" % b))
-            if m == FIRST_NARROW - 2:
+        for m, unit in enumerate(UNITS):
+            e, s, h = unit
+            cast(unit)
+            multiply(unit)
+            if unit == (0, 1, 1):
+                gathered(unit, 0, 2, 0)
+                gather_planes(2, over(unit, 1, [P, 2 * C], U8, "g_planes2"))
+            if unit == (1, 0, 1):
+                gathered(unit, 0, 2, 1)
+            if unit == (1, 1, 1):
+                gathered(unit, 0, 3, 0)
+                gather_planes(3, over(unit, 2, [P, 2 * C], U8, "g_planes3"))
+                gathered(unit, 1, 3, 1)
+            for k, b in empty_at.get(m, []):
+                empty(k, b)
+            if s is None and h > 0 and e != WIDE + 1:
+                r = max(1, e - WIDE)
+                prods[h - 1, r] = over(unit, 0, [P, T], F32, "prod%d_%d" % (h - 1, r))
+                fetch(h - 1, r, 0, T, prods[h - 1, r])
+            if s is None and e == E - 1 and h < BLOCKS - 1:
+                prods[h, 0] = over((WIDE, None, h), 1, [P, T], F32, "prod%d_0" % h)
+                fetch(h, 0, 0, T, prods[h, 0])
+            if unit in slope_after:
+                b = slope_after.index(unit)
+                u = over(unit, 0 if s is None else 3, [P, T], F32, "u%d" % b)
+                slope(b, u, over((0, 0, 0), b, [P, T // P, P], F32, "neg%d" % b))
+            if s is None and e == E - 1 and h > 0:
+                combine(h - 1, 0, T, [prods[h - 1, r] for r in range(TOP)])
+            if unit == BY_BLOCK[2][0]:
                 w1_grouped = keep.tile([P, K, 4], BF16, name="w1_grouped", align_bytes=64)
-                interleave(nc.vector.tensor_copy, w1_grouped[:], w1_raw[:])
+                interleave(nc.scalar.copy, w1_grouped[:], w1_raw[:])
                 w1q.extend(quantize(w1_grouped[:].rearrange("p k j -> p (k j)"), K, "w1", 1))
-            done, rest = divmod(m + 1 - FIRST_NARROW, narrow)
-            if m >= FIRST_NARROW and rest == 0:
-                if done >= 2:
-                    b = done - 2
-                    for r in range(2, TOP):
-                        prods[b, r] = over(m, r - 2, [P, T], F32, "prod%d_%d" % (b, r))
-                        fetch(b, r, 0, T, prods[b, r])
-                    combine(b, 0, T, [prods[b, r] for r in range(TOP)])
-                b = done - 1
-                if b < BLOCKS - 1:
-                    for r in range(2):
-                        prods[b, r] = over(20, 2 * (b % 2) + r, [P, T], F32, "prod%d_%d" % (b, r))
-                        fetch(b, r, 0, T, prods[b, r])
 
         for t0 in range(0, T, LAST_PIECE):
             last = []
             for r in range(TOP):
-                place = UNIT_BYTES * 18 + 4 * (T * r + t0)
-                last.append(stage.tile([P, LAST_PIECE], F32, name="last%d_%d" % (t0, r), offset=place, align_bytes=64))
+                spot = place((PROMPT, 0, 0)) + 4 * (T * r + t0)
+                last.append(stage.tile([P, LAST_PIECE], F32, name="last%d_%d" % (t0, r), offset=spot, align_bytes=64))
                 fetch(BLOCKS - 1, r, t0, LAST_PIECE, last[r])
             combine(BLOCKS - 1, t0, LAST_PIECE, last)
             finish(t0, LAST_PIECE, w1q[0], w1q[1])

@@ -27,12 +27,13 @@ PROMPT = 2
 NARROW = E - WIDE
 ROOM = 2048
 EMPTY_LAG = 2
-LAST_PIECE = 128
+LAST_PIECES = ((0, 256), (256, 128), (384, 128))
 FIRST = [(e, s, h) for e in range(WIDE) for s in range(PASSES) for h in range(2) if h == 0 or e < PROMPT]
 LATER = [(e, s, 1) for e in range(PROMPT, WIDE) for s in range(PASSES)]
 BY_BLOCK = [[(e, None, b) for e in range(WIDE, E)] for b in range(BLOCKS)]
 UNITS = FIRST + BY_BLOCK[0] + LATER + BY_BLOCK[1] + BY_BLOCK[2] + BY_BLOCK[3]
-VECTOR_CASTS = BY_BLOCK[0][::2]
+FETCH_AFTER = (WIDE + 1, E - 1, E - 1)
+VECTOR_CASTS = [(WIDE - 1, 0, 0)] + BY_BLOCK[0][::2] + LATER[::2]
 
 
 def tile_moe_sub_silu_kernel(
@@ -62,7 +63,7 @@ def tile_moe_sub_silu_kernel(
         gates = [keep.tile([P, T], F32, name="gates%d" % r) for r in range(TOP)]
         a_sb = [keep.tile([P, T], F32, name="a_sb%d" % b) for b in range(BLOCKS)]
         w1_raw = keep.tile([P, 4, K], F32, name="w1_raw")
-        da_t = keep.tile([P, T // P, H], BF16, name="da_t", align_bytes=64)
+        da_t = keep.tile([P, T // P * H], BF16, name="da_t", align_bytes=64)
 
         make_identity(nc, ident[:])
         nc.vector.memset(planes[:].bitcast(I32), 0)
@@ -135,18 +136,14 @@ def tile_moe_sub_silu_kernel(
             nc.vector.tensor_copy(dst[:], planes[:].indirect(offs_sb[:, 32 * k : 32 * (k + 1)]))
             g_planes[k] = dst
 
-        grouped = {}
-
-        def cast(unit):
+        def cast(unit, dst):
             e, s, h = unit
-            dst = ring.tile([P, 2 * P, 4], BF16, name="grouped", tag="grouped", bufs=8, align_bytes=64)
             engine_copy = nc.vector.tensor_copy if unit in VECTOR_CASTS else nc.scalar.copy
             if s is None:
                 src = raw[unit][:].rearrange("p j s w -> p j (s w)")
             else:
                 src = raw[e, s][:, :, 2 * P * h : 2 * P * (h + 1)]
-            interleave(engine_copy, dst[:], src)
-            grouped[unit] = dst
+            interleave(engine_copy, dst, src)
 
         def quantize(src, cols, tag, bufs):
             codes = ring.tile([P, cols], U32, name="codes", tag="codes" + tag, bufs=bufs, align_bytes=64)
@@ -163,8 +160,8 @@ def tile_moe_sub_silu_kernel(
                 accs[k, b] = psum.tile([P, 2 * C], F32, name="acc", tag="acc", bufs=6)
             slots = slice(C * half, C * (half + 1))
             for s in range(PASSES):
-                codes, scales, col = operands[s]
-                cols = slice(P * col, P * (col + 1))
+                codes, scales, first, col = operands[s]
+                cols = slice(P * (first + col), P * (first + col + 1))
                 nc.tensor.matmul_mx(
                     accs[k, b][:, slots],
                     lhsT=codes[:, cols].bitcast(FP8X4),
@@ -180,14 +177,16 @@ def tile_moe_sub_silu_kernel(
 
         quantized = {}
 
-        def multiply(unit):
-            e, s, h = unit
-            quantized[unit] = quantize(grouped[unit][:].rearrange("p w j -> p (w j)"), 2 * P, "w2", 6)
-            if s is None:
-                expert(e, h, [quantized[unit] + (t,) for t in range(PASSES)])
-            elif s == PASSES - 1:
-                for i in range(2):
-                    expert(e, 2 * h + i, [quantized[e, t, h] + (i,) for t in range(PASSES)])
+        def multiply(units, grouped):
+            codes, scales = quantize(grouped[:].rearrange("p w j -> p (w j)"), 4 * P, "w2", 3)
+            for i, unit in enumerate(units):
+                quantized[unit] = (codes, scales, 2 * i)
+            for e, s, h in units:
+                if s is None:
+                    expert(e, h, [quantized[e, s, h] + (t,) for t in range(PASSES)])
+                elif s == PASSES - 1:
+                    for i in range(2):
+                        expert(e, 2 * h + i, [quantized[e, t, h] + (i,) for t in range(PASSES)])
 
         def fetch(b, r, t0, nt, prod):
             nc.vector.tensor_tensor(
@@ -204,13 +203,13 @@ def tile_moe_sub_silu_kernel(
                     )
             blocks = slice(t0 // P, (t0 + nt) // P)
             nc.vector.scalar_tensor_tensor(
-                da_t[:, blocks, P * b : P * (b + 1)], dh[:], -1.0, slopes[b][:, blocks, :], MULT, MULT
+                da_t[:].rearrange("p (tb i) -> p tb i", i=H)[:, blocks, P * b : P * (b + 1)], dh[:], -1.0, slopes[b][:, blocks, :], MULT, MULT
             )
 
         def finish(t0, nt, w1_codes, w1_scales):
             back = psum.tile([P, nt // P, 2, P], F32, name="back", tag="acc", bufs=6)
             for tb in range(nt // P):
-                pairs = da_t[:, t0 // P + tb, :].bitcast(F32)
+                pairs = da_t[:, H * (t0 // P + tb) : H * (t0 // P + tb + 1)].bitcast(F32)
                 for u in range(2):
                     nc.tensor.transpose(back[:, tb, u, :], pairs[:, u::2], ident[:])
             da = ring.tile([P, nt // P, P, 4], BF16, name="da", tag="da", bufs=2, align_bytes=64)
@@ -247,8 +246,11 @@ def tile_moe_sub_silu_kernel(
         w1q = []
         for m, unit in enumerate(UNITS):
             e, s, h = unit
-            cast(unit)
-            multiply(unit)
+            if m % 2 == 0:
+                grouped = ring.tile([P, 4 * P, 4], BF16, name="grouped", tag="grouped", bufs=4, align_bytes=64)
+            cast(unit, grouped[:, 2 * P * (m % 2) : 2 * P * (m % 2 + 1), :])
+            if m % 2 == 1:
+                multiply(UNITS[m - 1 : m + 1], grouped)
             if unit == (0, 1, 1):
                 gathered(unit, 0, 2, 0)
                 gather_planes(2, over(unit, 1, [P, 2 * C], U8, "g_planes2"))
@@ -260,12 +262,12 @@ def tile_moe_sub_silu_kernel(
                 gathered(unit, 1, 3, 1)
             for k, b in empty_at.get(m, []):
                 empty(k, b)
-            if s is None and h > 0 and e != WIDE + 1:
-                r = max(1, e - WIDE)
-                prods[h - 1, r] = over(unit, 0, [P, T], F32, "prod%d_%d" % (h - 1, r))
-                fetch(h - 1, r, 0, T, prods[h - 1, r])
+            for r in range(1, TOP):
+                if s is None and h > 0 and e == FETCH_AFTER[r - 1]:
+                    prods[h - 1, r] = over(unit, r % 2, [P, T], F32, "prod%d_%d" % (h - 1, r))
+                    fetch(h - 1, r, 0, T, prods[h - 1, r])
             if s is None and e == E - 1 and h < BLOCKS - 1:
-                prods[h, 0] = over((WIDE, None, h), 1, [P, T], F32, "prod%d_0" % h)
+                prods[h, 0] = over((E - 2, None, h), 1, [P, T], F32, "prod%d_0" % h)
                 fetch(h, 0, 0, T, prods[h, 0])
             if unit in slope_after:
                 b = slope_after.index(unit)
@@ -278,11 +280,10 @@ def tile_moe_sub_silu_kernel(
                 interleave(nc.scalar.copy, w1_grouped[:], w1_raw[:])
                 w1q.extend(quantize(w1_grouped[:].rearrange("p k j -> p (k j)"), K, "w1", 1))
 
-        for t0 in range(0, T, LAST_PIECE):
+        for t0, nt in LAST_PIECES:
             last = []
             for r in range(TOP):
-                spot = place((PROMPT, 0, 0)) + 4 * (T * r + t0)
-                last.append(stage.tile([P, LAST_PIECE], F32, name="last%d_%d" % (t0, r), offset=spot, align_bytes=64))
-                fetch(BLOCKS - 1, r, t0, LAST_PIECE, last[r])
-            combine(BLOCKS - 1, t0, LAST_PIECE, last)
-            finish(t0, LAST_PIECE, w1q[0], w1q[1])
+                last.append(over((PROMPT, 0, 0), r, [P, nt], F32, "last%d_%d" % (t0, r)))
+                fetch(BLOCKS - 1, r, t0, nt, last[r])
+            combine(BLOCKS - 1, t0, nt, last)
+            finish(t0, nt, w1q[0], w1q[1])

from contextlib import ExitStack

import concourse.mybir as mybir
from concourse.masks import make_identity

K, T, E, C, H, N, TOP = 128, 512, 8, 256, 512, 1024, 4
S = E * C
FLOPS = 2 * N * H * S + 2 * H * K * T

F32 = mybir.dt.float32
BF16 = mybir.dt.bfloat16
I32 = mybir.dt.int32
U32 = mybir.dt.uint32
U16 = mybir.dt.uint16
U8 = mybir.dt.uint8
FP8X4 = mybir.dt.float8_e4m3fn_x4
MULT = mybir.AluOpType.mult
SUB = mybir.AluOpType.subtract
SIGMOID = mybir.ActivationFunctionType.Sigmoid

P = 128
PASSES = N // (4 * P)
BLOCKS = H // P
SPARE = 256
WIDE = 4
PROMPT = 2
NARROW = E - WIDE
ROOM = 2048
EMPTY_LAG = 2
LAST_PIECES = ((0, 256), (256, 128), (384, 128))
FIRST = [(e, s, h) for e in range(WIDE) for s in range(PASSES) for h in range(2) if h == 0 or e < PROMPT]
LATER = [(e, s, 1) for e in range(PROMPT, WIDE) for s in range(PASSES)]
BY_BLOCK = [[(e, None, b) for e in range(WIDE, E)] for b in range(BLOCKS)]
UNITS = FIRST + BY_BLOCK[0] + LATER + BY_BLOCK[1] + BY_BLOCK[2] + BY_BLOCK[3]
FETCH_AFTER = (WIDE + 1, E - 1, E - 1)
VECTOR_CASTS = [(WIDE - 1, 0, 0)] + BY_BLOCK[0][::2] + LATER[::2]


def tile_moe_sub_silu_kernel(
    tc, dy_words, dy_scales, w2t, w1t, a, gate, offs, pos1, pos2, pos3, pos4, out
):
    nc = tc.nc
    with ExitStack() as ctx:
        keep = ctx.enter_context(tc.tile_pool(name="keep", bufs=1))
        stage = ctx.enter_context(tc.tile_pool(name="stage", bufs=1))
        ring = ctx.enter_context(tc.tile_pool(name="ring", bufs=1))
        psum = ctx.enter_context(tc.psum_pool(name="psum", bufs=1))

        def place(unit):
            e, s, h = unit
            if s is None:
                return 4 * ROOM * PASSES * WIDE + 2 * ROOM * (NARROW * h + e - WIDE)
            return 4 * ROOM * (PASSES * e + s)

        def over(unit, room, shape, dtype, name):
            return stage.tile(shape, dtype, name=name, offset=place(unit) + ROOM * room, align_bytes=64)

        offs_sb = keep.tile([P, S // 16], U16, name="offs_sb")
        pos_sb = [keep.tile([P, T // 16], U16, name="pos_sb%d" % r) for r in range(TOP)]
        words = [keep.tile([P, T + SPARE], I32, name="words%d" % s, align_bytes=64) for s in range(PASSES)]
        planes = keep.tile([P, 2 * T], U8, name="planes", align_bytes=64)
        ident = keep.tile([P, P], F32, name="ident")
        gates = [keep.tile([P, T], F32, name="gates%d" % r) for r in range(TOP)]
        a_sb = [keep.tile([P, T], F32, name="a_sb%d" % b) for b in range(BLOCKS)]
        w1_raw = keep.tile([P, 4, K], F32, name="w1_raw")
        da_t = keep.tile([P, T // P * H], BF16, name="da_t", align_bytes=64)

        make_identity(nc, ident[:])
        nc.vector.memset(planes[:].bitcast(I32), 0)
        for s in range(PASSES):
            nc.vector.memset(words[s][:, T:], 0)

        nc.sync.dma_start(offs_sb[:], offs)
        for s in range(PASSES):
            nc.sync.dma_start(words[s][:, :T], dy_words[s].rearrange("p t d -> p (t d)").bitcast(I32))
        raw = {}
        for e in range(WIDE):
            for s in range(PASSES):
                raw[e, s] = over((e, s, 0), 0, [P, 4, H], F32, "raw%d_%d" % (e, s))
                rows = w2t[e, 4 * P * s : 4 * P * (s + 1), :]
                nc.sync.dma_start(raw[e, s][:], rows.rearrange("(p j) w -> p j w", j=4))
                n = PASSES * e + s
                if n == 0:
                    for q in range(4):
                        nc.sync.dma_start(
                            planes[32 * q : 32 * q + 4 * PASSES, :T].bitcast(I32),
                            dy_scales[:, 4 * q : 4 * (q + 1), :].bitcast(I32),
                        )
                b = n - 3
                if 0 <= b < BLOCKS:
                    nc.sync.dma_start(a_sb[b][:], a[P * b : P * (b + 1), :])
        for b in range(BLOCKS):
            for e in range(WIDE, E):
                raw[e, None, b] = over((e, None, b), 0, [P, 4, PASSES, P], F32, "raw%d_b%d" % (e, b))
                for s in range(PASSES):
                    rows = w2t[e, 4 * P * s : 4 * P * (s + 1), P * b : P * (b + 1)]
                    nc.sync.dma_start(raw[e, None, b][:, :, s, :], rows.rearrange("(p j) w -> p j w", j=4))
                if (b, e) == (0, E - 1):
                    for r, pos in enumerate((pos1, pos2, pos3, pos4)):
                        nc.sync.dma_start(pos_sb[r][:], pos)
                    nc.sync.dma_start(gates[0][:], gate[0])
                if (b, e) == (1, WIDE):
                    for r in range(1, TOP):
                        nc.sync.dma_start(gates[r][:], gate[r])
                if (b, e) == (1, WIDE + 1):
                    nc.sync.dma_start(w1_raw[:], w1t.rearrange("(p j) k -> p j k", j=4))

        def interleave(engine_copy, dst, src):
            engine_copy(
                dst.rearrange("p (c i) j -> p c j i", i=4),
                src.rearrange("p j (c i) -> p c j i", i=4),
            )

        slopes = {}

        def slope(b, u, neg):
            a_t = psum.tile([P, T // P, P], F32, name="a_t", tag="turn", bufs=2)
            for tb in range(T // P):
                nc.tensor.transpose(a_t[:, tb, :], a_sb[b][:, P * tb : P * (tb + 1)], ident[:])
            v = a_t[:].rearrange("p b i -> p (b i)")
            sg = ring.tile([P, T], F32, name="sg", tag="sg", bufs=2)
            nc.scalar.activation(sg[:], v, SIGMOID)
            nc.vector.scalar_tensor_tensor(u[:], sg[:], 1.0, v, SUB, MULT)
            nc.vector.scalar_tensor_tensor(neg[:].rearrange("p b i -> p (b i)"), u[:], 1.0, sg[:], SUB, MULT)
            slopes[b] = neg

        g_words = {}
        g_planes = {}

        def gather_words(k, s, dst):
            window = words[s][:].bitcast(U32)
            nc.vector.tensor_copy(dst[:], window.indirect(offs_sb[:, 32 * k : 32 * (k + 1)]))
            g_words[k, s] = dst

        def gather_planes(k, dst):
            nc.vector.tensor_copy(dst[:], planes[:].indirect(offs_sb[:, 32 * k : 32 * (k + 1)]))
            g_planes[k] = dst

        def cast(unit, dst):
            e, s, h = unit
            engine_copy = nc.vector.tensor_copy if unit in VECTOR_CASTS else nc.scalar.copy
            if s is None:
                src = raw[unit][:].rearrange("p j s w -> p j (s w)")
            else:
                src = raw[e, s][:, :, 2 * P * h : 2 * P * (h + 1)]
            interleave(engine_copy, dst, src)

        def quantize(src, cols, tag, bufs):
            codes = ring.tile([P, cols], U32, name="codes", tag="codes" + tag, bufs=bufs, align_bytes=64)
            scales = ring.tile([P, cols], U8, name="scales", tag="scales" + tag, bufs=bufs, align_bytes=64)
            nc.vector.quantize_mx(codes[:].bitcast(FP8X4), scales[:], src)
            return codes, scales

        accs = {}
        ys = [keep.tile([P, S], F32, name="y%d" % b) for b in range(BLOCKS)]

        def expert(e, b, operands):
            k, half = divmod(e, 2)
            if half == 0:
                accs[k, b] = psum.tile([P, 2 * C], F32, name="acc", tag="acc", bufs=6)
            slots = slice(C * half, C * (half + 1))
            for s in range(PASSES):
                codes, scales, first, col = operands[s]
                cols = slice(P * (first + col), P * (first + col + 1))
                nc.tensor.matmul_mx(
                    accs[k, b][:, slots],
                    lhsT=codes[:, cols].bitcast(FP8X4),
                    lhsT_scale=scales[:, cols],
                    rhs=g_words[k, s][:, slots].bitcast(FP8X4),
                    rhs_scale=g_planes[k][4 * s :, slots],
                    start=(s == 0),
                    stop=(s == PASSES - 1),
                )

        def empty(k, b):
            nc.scalar.copy(ys[b][:, 2 * C * k : 2 * C * (k + 1)], accs[k, b][:])

        quantized = {}

        def multiply(units, grouped):
            codes, scales = quantize(grouped[:].rearrange("p w j -> p (w j)"), 4 * P, "w2", 3)
            for i, unit in enumerate(units):
                quantized[unit] = (codes, scales, 2 * i)
            for e, s, h in units:
                if s is None:
                    expert(e, h, [quantized[e, s, h] + (t,) for t in range(PASSES)])
                elif s == PASSES - 1:
                    for i in range(2):
                        expert(e, 2 * h + i, [quantized[e, t, h] + (i,) for t in range(PASSES)])

        def fetch(b, r, t0, nt, prod):
            nc.vector.tensor_tensor(
                prod[:], ys[b][:].indirect(pos_sb[r][:, t0 // 16 : (t0 + nt) // 16]), gates[r][:, t0 : t0 + nt], MULT
            )

        def combine(b, t0, nt, prods):
            dh = psum.tile([P, nt // P, P], F32, name="dh", tag="turn", bufs=2)
            for tb in range(nt // P):
                for r in range(TOP):
                    nc.tensor.matmul(
                        dh[:, tb, :], prods[r][:, P * tb : P * (tb + 1)], ident[:],
                        start=(r == 0), stop=(r == TOP - 1), is_transpose=True,
                    )
            blocks = slice(t0 // P, (t0 + nt) // P)
            nc.vector.scalar_tensor_tensor(
                da_t[:].rearrange("p (tb i) -> p tb i", i=H)[:, blocks, P * b : P * (b + 1)], dh[:], -1.0, slopes[b][:, blocks, :], MULT, MULT
            )

        def finish(t0, nt, w1_codes, w1_scales):
            back = psum.tile([P, nt // P, 2, P], F32, name="back", tag="acc", bufs=6)
            for tb in range(nt // P):
                pairs = da_t[:, H * (t0 // P + tb) : H * (t0 // P + tb + 1)].bitcast(F32)
                for u in range(2):
                    nc.tensor.transpose(back[:, tb, u, :], pairs[:, u::2], ident[:])
            da = ring.tile([P, nt // P, P, 4], BF16, name="da", tag="da", bufs=2, align_bytes=64)
            flat = da[:].rearrange("p b t j -> p (b t j)")
            nc.scalar.copy(
                flat.bitcast(F32).rearrange("p (b t u) -> p b t u", u=2, t=P), back[:].rearrange("p b u t -> p b t u")
            )
            codes, scales = quantize(flat, nt, "da", 2)
            res = psum.tile([P, nt], F32, name="res", tag="acc", bufs=6)
            nc.tensor.matmul_mx(
                res[:], lhsT=w1_codes[:].bitcast(FP8X4), lhsT_scale=w1_scales[:],
                rhs=codes[:].bitcast(FP8X4), rhs_scale=scales[:], start=True, stop=True,
            )
            res_sb = ring.tile([P, nt], F32, name="res_sb", tag="res_sb", bufs=4)
            nc.scalar.copy(res_sb[:], res[:])
            nc.sync.dma_start(out[:, t0 : t0 + nt], res_sb[:])

        for k in range(2):
            for s in range(PASSES):
                gather_words(k, s, keep.tile([P, 2 * C], U32, name="g_words%d_%d" % (k, s), align_bytes=64))
            gather_planes(k, keep.tile([P, 2 * C], U8, name="g_planes%d" % k, align_bytes=64))

        def gathered(unit, room, k, s):
            gather_words(k, s, over(unit, room, [P, 2 * C], U32, "g_words%d_%d" % (k, s)))

        empty_at = {}
        for m, (e, s, h) in enumerate(UNITS):
            if e % 2 == 1 and s is None:
                empty_at.setdefault(m, []).append((e // 2, h))
            if e % 2 == 1 and s == PASSES - 1:
                empty_at.setdefault(m + EMPTY_LAG, []).extend([(e // 2, 2 * h), (e // 2, 2 * h + 1)])
        slope_after = [(1, 1, 1), BY_BLOCK[0][0], BY_BLOCK[0][1], BY_BLOCK[0][-1]]
        prods = {}
        w1q = []
        for m, unit in enumerate(UNITS):
            e, s, h = unit
            if m % 2 == 0:
                grouped = ring.tile([P, 4 * P, 4], BF16, name="grouped", tag="grouped", bufs=4, align_bytes=64)
            cast(unit, grouped[:, 2 * P * (m % 2) : 2 * P * (m % 2 + 1), :])
            if m % 2 == 1:
                multiply(UNITS[m - 1 : m + 1], grouped)
            if unit == (0, 1, 1):
                gathered(unit, 0, 2, 0)
                gather_planes(2, over(unit, 1, [P, 2 * C], U8, "g_planes2"))
            if unit == (1, 0, 1):
                gathered(unit, 0, 2, 1)
            if unit == (1, 1, 1):
                gathered(unit, 0, 3, 0)
                gather_planes(3, over(unit, 2, [P, 2 * C], U8, "g_planes3"))
                gathered(unit, 1, 3, 1)
            for k, b in empty_at.get(m, []):
                empty(k, b)
            for r in range(1, TOP):
                if s is None and h > 0 and e == FETCH_AFTER[r - 1]:
                    prods[h - 1, r] = over(unit, r % 2, [P, T], F32, "prod%d_%d" % (h - 1, r))
                    fetch(h - 1, r, 0, T, prods[h - 1, r])
            if s is None and e == E - 1 and h < BLOCKS - 1:
                prods[h, 0] = over((E - 2, None, h), 1, [P, T], F32, "prod%d_0" % h)
                fetch(h, 0, 0, T, prods[h, 0])
            if unit in slope_after:
                b = slope_after.index(unit)
                u = over(unit, 0 if s is None else 3, [P, T], F32, "u%d" % b)
                slope(b, u, over((0, 0, 0), b, [P, T // P, P], F32, "neg%d" % b))
            if s is None and e == E - 1 and h > 0:
                combine(h - 1, 0, T, [prods[h - 1, r] for r in range(TOP)])
            if unit == BY_BLOCK[2][0]:
                w1_grouped = keep.tile([P, K, 4], BF16, name="w1_grouped", align_bytes=64)
                interleave(nc.scalar.copy, w1_grouped[:], w1_raw[:])
                w1q.extend(quantize(w1_grouped[:].rearrange("p k j -> p (k j)"), K, "w1", 1))

        for t0, nt in LAST_PIECES:
            last = []
            for r in range(TOP):
                last.append(over((PROMPT, 0, 0), r, [P, nt], F32, "last%d_%d" % (t0, r)))
                fetch(BLOCKS - 1, r, t0, nt, last[r])
            combine(BLOCKS - 1, t0, nt, last)
            finish(t0, nt, w1q[0], w1q[1])
